import numpy as np
import ml_dtypes


def mxq(x, axis, fmt="e4m3"):
    dtype, down = {"e4m3": (ml_dtypes.float8_e4m3fn, 7), "e5m2": (ml_dtypes.float8_e5m2, 14)}[fmt]
    v = np.moveaxis(np.asarray(x, np.float32).astype(ml_dtypes.bfloat16).astype(np.float64), axis, -1)
    blocks = v.reshape(v.shape[:-1] + (-1, 32))
    amax = np.abs(blocks).max(-1, keepdims=True)
    byte = np.maximum(np.where(amax > 0, np.frexp(amax)[1] - 1 + 127, 0) - down, 1)
    scale = np.exp2(byte - 127.0)
    codes = (blocks / scale).astype(np.float32).astype(dtype).astype(np.float64)
    return np.moveaxis((codes * scale).reshape(v.shape), -1, axis)


WIDE = False


def mx_kscale(k):
    if not WIDE:
        return np.ones(k)
    levels = np.array([10, -10, 5, -5, 0])
    if k % 512:
        return np.exp2(np.random.permutation(np.resize(levels, k // 32))).repeat(32)
    a = np.empty((k // 512, 16))
    for p in range(k // 512):
        a[p, :8] = np.random.permutation(np.resize(levels, 8))
        for g in range(8):
            far = levels[np.abs(levels - a[p, g]) >= 10]
            a[p, g + 8] = far[np.random.randint(len(far))]
    return np.exp2(a.ravel()).repeat(32)


BF16 = ml_dtypes.bfloat16


def bf(x):
    return np.asarray(x, np.float32).astype(BF16)


def f64(x):
    return np.asarray(x).astype(np.float64)


E2M1 = np.array([0.0, 0.5, 1.0, 1.5, 2.0, 3.0, 4.0, 6.0, -0.0, -0.5, -1.0, -1.5, -2.0, -3.0, -4.0, -6.0])


def pack_weight(w, fmt):
    k, n = w.shape
    w = f64(bf(w)).reshape(k // 32, 32, n)
    amax = np.abs(w).max(1)
    if fmt == "e4m3":
        byte = np.frexp(amax)[1] - 1 + 127 - 7
    else:
        mant, ex = np.frexp(amax / 6.0)
        byte = np.where(mant > 0.5, ex, ex - 1) + 127
    byte = np.clip(np.where(amax > 0, byte, 1), 1, 254)
    scaled = (w * np.exp2(127.0 - byte)[:, None, :]).reshape(k, n).astype(np.float32)
    by_word = np.ascontiguousarray(scaled.reshape(k // 512, 128, 4, n).transpose(0, 1, 3, 2))
    if fmt == "e4m3":
        words = by_word.astype(ml_dtypes.float8_e4m3fn).view(np.uint8)
    else:
        c = by_word.astype(ml_dtypes.float4_e2m1fn).view(np.uint8) & 0xF
        words = c[..., 0::2] | (c[..., 1::2] << 4)
    return np.ascontiguousarray(words), np.ascontiguousarray(byte.astype(np.uint8).reshape(k // 512, 16, n))


def unpack_weight(words, scales, fmt):
    g, p, n, _ = words.shape
    if fmt == "e4m3":
        vals = np.ascontiguousarray(words).view(ml_dtypes.float8_e4m3fn).astype(np.float64)
    else:
        nib = np.empty((g, p, n, 4), np.uint8)
        nib[..., 0::2] = words & 0xF
        nib[..., 1::2] = words >> 4
        vals = E2M1[nib]
    vals = vals * np.repeat(np.exp2(scales.astype(np.float64) - 127.0), 8, axis=1)[..., None]
    return vals.transpose(0, 1, 3, 2).reshape(g * 512, n)
def pack4(w):
    words, scales = pack_weight(w, "e2m1")
    return words.reshape(words.shape[0], 128, -1), scales


def unpack4(words, scales):
    return unpack_weight(words.reshape(words.shape[0], 128, -1, 2), scales, "e2m1")


def planes(Y):
    n, m = Y.shape
    b = f64(bf(Y)).reshape(n // 32, 32, m)
    amax = np.abs(b).max(1)
    byte = np.clip(np.where(amax > 0, np.frexp(amax)[1] - 1 + 127 - 7, 1), 1, 254)
    codes = (b * np.exp2(127.0 - byte)[:, None, :]).reshape(n, m).astype(np.float32).astype(ml_dtypes.float8_e4m3fn).view(np.uint8)
    words = codes.reshape(n // 512, 128, 4, m).transpose(0, 1, 3, 2)
    return np.ascontiguousarray(words), np.ascontiguousarray(byte.astype(np.uint8).reshape(n // 512, 16, m))


R, P, V = 512, 1536, 2048

def setup_inputs():
    s = mx_kscale(P)[:, None]
    strength = np.exp(0.8 * np.random.randn(V))[None, :]
    z = np.random.randn(P, R) * s
    c = np.random.randn(P, V) * strength / np.sqrt(P) / s
    b = np.random.randn(P, V) * strength / np.sqrt(P) / s
    d = np.random.randn(P, V) * strength / np.sqrt(P) / s
    z_words, z_scales = pack_weight(z, "e4m3")
    b_words, b_scales = pack4(b)
    d_words, d_scales = pack_weight(d, "e4m3")
    gap = np.exp(0.4 * np.random.randn(V))
    lam = 0.4 + 0.6 * np.random.rand(R)
    return {"z_words": z_words, "z_scales": z_scales, "c": bf(c),
            "b_words": b_words, "b_scales": b_scales,
            "d_words": d_words, "d_scales": d_scales,
            "gap": bf(gap), "lam": bf(lam)}

def reference(z_words, z_scales, c, b_words, b_scales, d_words, d_scales, gap, lam):
    z = unpack_weight(z_words, z_scales, "e4m3")
    b = unpack4(b_words, b_scales)
    d = unpack_weight(d_words, d_scales, "e4m3")
    amp = z.T @ mxq(f64(c), 0, "e4m3")
    exch = z.T @ b
    direct = z.T @ d
    y = f64(gap)[None, :] * amp + f64(lam)[:, None] * (exch - direct)
    Y = y.T
    words, scales = planes(Y)
    return y, words, scales

@@ -1,0 +1,328 @@
+from contextlib import ExitStack
+
+import concourse.mybir as mybir
+from concourse.masks import make_identity
+
+R, K, V = 512, 1536, 2048
+FLOPS = 3 * 2 * R * K * V
+
+F32 = mybir.dt.float32
+BF16 = mybir.dt.bfloat16
+I32 = mybir.dt.int32
+U32 = mybir.dt.uint32
+U8 = mybir.dt.uint8
+FP8X4 = mybir.dt.float8_e4m3fn_x4
+FP4X4 = mybir.dt.float4_e2m1fn_x4
+ALU = mybir.AluOpType
+
+P = 128
+PACK = 4
+PASSES = K // (P * PACK)
+CHUNK = 512
+CHUNKS = V // CHUNK
+TILES = R // P
+QUADS = 4
+BANKS = 8
+RUN = 4
+VECTOR_COLUMNS = (320, 192, 64, 64)
+
+
+def tile_gap_scaled_pair_action_k3_kernel(
+    tc, z_words, z_scales, c, b_words, b_scales, d_words, d_scales, gap, lam, out_0, out_1, out_2
+):
+    nc = tc.nc
+    with ExitStack() as ctx:
+        keep = ctx.enter_context(tc.tile_pool(name="keep", bufs=1))
+        work = ctx.enter_context(tc.tile_pool(name="work", bufs=3))
+        psum = ctx.enter_context(tc.psum_pool(name="psum", bufs=1))
+        ctx.enter_context(tc.manual_schedule())
+
+        def kept(name, shape, dtype):
+            return keep.tile(shape, dtype, name=name, align_bytes=64)
+
+        def columns(g):
+            return slice(g * CHUNK, (g + 1) * CHUNK)
+
+        def rows(i):
+            return slice(i * P, (i + 1) * P)
+
+        def scale_plane(name, width):
+            plane = kept(name, [P, PASSES, width], U8)
+            nc.vector.memset(plane[:].bitcast(U32), 0)
+            return plane
+
+        def load_scales(plane, scales, cols):
+            for q in range(QUADS):
+                nc.sync.dma_start(
+                    out=plane[32 * q : 32 * q + 4, :, :].bitcast(I32),
+                    in_=scales[:, 4 * q : 4 * q + 4, cols].rearrange("j r n -> r j n").bitcast(I32),
+                )
+
+        z_plane = scale_plane("z_plane", R)
+        b_plane = {0: scale_plane("b_plane0", CHUNK)}
+        d_plane = kept("d_plane", [P, V], U8)
+        nc.vector.memset(d_plane[:].bitcast(U32), 0)
+        for g in range(1, CHUNKS):
+            b_plane[g] = scale_plane("b_plane%d" % g, CHUNK)
+        identity = kept("identity", [P, P], F32)
+        make_identity(nc, identity[:])
+
+        z_sb, d_sb, b_sb, c_raw, gap_sb = {}, {}, {}, {}, {}
+        z_view = z_words.rearrange("j p n t -> p j (n t)")
+        d_view = d_words.rearrange("j p n t -> p j (n t)")
+        b_view = b_words.rearrange("j p n -> p j n")
+
+        def load_z(j):
+            z_sb[j] = kept("z%d" % j, [P, R], U32)
+            nc.sync.dma_start(out=z_sb[j][:].bitcast(I32), in_=z_view[:, j, :].bitcast(I32))
+
+        def load_d(g):
+            d_sb[g] = kept("d%d" % g, [P, PASSES, CHUNK], U32)
+            src = d_view[:, :, g * CHUNK * PACK : (g + 1) * CHUNK * PACK]
+            nc.sync.dma_start(out=d_sb[g][:].bitcast(I32), in_=src.bitcast(I32))
+
+        def load_b(g, j0, j1):
+            words = kept("b%d_%d" % (g, j0), [P, j1 - j0, 2 * CHUNK], U8)
+            src = b_view[:, j0:j1, g * 2 * CHUNK : (g + 1) * 2 * CHUNK]
+            nc.sync.dma_start(out=words[:].bitcast(I32), in_=src.bitcast(I32))
+            for j in range(j0, j1):
+                b_sb[g, j] = words[:, j - j0, :]
+
+        def load_c(g, j):
+            c_raw[g, j] = kept("c%d_%d" % (g, j), [P, PACK, CHUNK], BF16)
+            src = c[j * P * PACK : (j + 1) * P * PACK, columns(g)].rearrange("(p t) v -> p t v", t=PACK)
+            nc.sync.dma_start(out=c_raw[g, j][:], in_=src)
+
+        def load_gap(g):
+            gap_sb[g] = kept("gap%d" % g, [P, CHUNK], BF16)
+            nc.sync.dma_start(out=gap_sb[g][:], in_=gap[columns(g)].partition_broadcast(P))
+
+        load_z(0)
+        load_b(0, 0, 1)
+        load_scales(z_plane, z_scales, slice(0, R))
+        load_scales(b_plane[0], b_scales, columns(0))
+        load_z(1)
+        load_b(0, 1, PASSES)
+        load_c(0, 0)
+        load_z(2)
+        load_c(0, 1)
+        load_c(0, 2)
+        load_gap(0)
+        lam_sb = kept("lam_sb", [P, TILES, 2], BF16)
+        with nc.allow_non_contiguous_dma(reason="one coupling strength for each partition"):
+            nc.sync.dma_start(out=lam_sb[:, :, 0:1], in_=lam.rearrange("(i p o) -> p i o", p=P, o=1))
+        for q in range(QUADS):
+            nc.sync.dma_start(
+                out=d_plane[32 * q : 32 * q + 4 * PASSES, :].bitcast(I32),
+                in_=d_scales[:, 4 * q : 4 * q + 4, :].bitcast(I32),
+            )
+        load_d(0)
+        for g in range(1, CHUNKS):
+            load_scales(b_plane[g], b_scales, columns(g))
+            load_b(g, 0, PASSES)
+            for j in range(PASSES):
+                load_c(g, j)
+            load_gap(g)
+            load_d(g)
+
+        grouped, c_codes, c_plane = {}, {}, {}
+
+        def interleave(engine_copy, g, j, lo, hi):
+            if (g, j) not in grouped:
+                grouped[g, j] = work.tile([P, CHUNK, PACK], BF16, name="grouped", bufs=4, align_bytes=64)
+            engine_copy(
+                out=grouped[g, j][:, lo:hi, :].rearrange("p (a i) t -> p a t i", i=RUN),
+                in_=c_raw[g, j][:, :, lo:hi].rearrange("p t (a i) -> p a t i", i=RUN),
+            )
+
+        def interleave_scalar(g, j):
+            interleave(nc.scalar.copy, g, j, VECTOR_COLUMNS[g], CHUNK)
+
+        def interleave_vector(g, j):
+            interleave(nc.vector.tensor_copy, g, j, 0, VECTOR_COLUMNS[g])
+
+        def quantise_c(g, j):
+            c_codes[g, j] = kept("c_codes%d_%d" % (g, j), [P, CHUNK], U32)
+            c_plane[g, j] = kept("c_plane%d_%d" % (g, j), [P, CHUNK], U8)
+            nc.vector.quantize_mx(
+                out=c_codes[g, j][:].bitcast(FP8X4),
+                scales=c_plane[g, j][:],
+                in_=grouped[g, j][:].rearrange("p v t -> p (v t)"),
+            )
+
+        free = list(range(BANKS))
+        held = {}
+
+        def take_bank(key, shape):
+            n = free[0]
+            free.remove(n)
+            held[key] = (n, psum.tile(shape, F32, name="bank%d" % n))
+            return held[key][1]
+
+        def release_bank(key):
+            free.append(held[key][0])
+
+        def moving(kind, g, j):
+            if kind == "amp":
+                return c_codes[g, j][:].bitcast(FP8X4), c_plane[g, j][:]
+            if kind == "direct":
+                return d_sb[g][:, j, :].bitcast(FP8X4), d_plane[4 * j :, columns(g)]
+            return b_sb[g, j].bitcast(FP4X4), b_plane[g][:, j, :]
+
+        def mx_pass(kind, g, i, j):
+            acc = take_bank((kind, g, i), [P, CHUNK]) if j == 0 else held[kind, g, i][1]
+            codes, plane = moving(kind, g, j)
+            nc.tensor.matmul_mx(
+                out=acc[:],
+                lhsT=z_sb[j][:, rows(i)].bitcast(FP8X4),
+                lhsT_scale=z_plane[:, j, rows(i)],
+                rhs=codes,
+                rhs_scale=plane,
+                start=(j == 0),
+                stop=(j == PASSES - 1),
+            )
+
+        def product(kind, g, i):
+            for j in range(PASSES):
+                mx_pass(kind, g, i, j)
+
+        scaled, partial, y_sb, y_pairs, y_grouped, y_codes = {}, {}, {}, {}, {}, {}
+        y_plane = kept("y_plane", [P, R], U8)
+
+        def take_amp(g, i):
+            scaled[g, i] = work.tile([P, CHUNK], F32, name="scaled")
+            nc.vector.tensor_tensor(out=scaled[g, i][:], in0=held["amp", g, i][1][:], in1=gap_sb[g][:], op=ALU.mult)
+            release_bank(("amp", g, i))
+
+        def take_exch(g, i):
+            partial[g, i] = work.tile([P, CHUNK], F32, name="partial", bufs=4)
+            nc.vector.scalar_tensor_tensor(
+                out=partial[g, i][:], in0=held["exch", g, i][1][:], scalar=lam_sb[:, i, 0:1],
+                in1=scaled[g, i][:], op0=ALU.mult, op1=ALU.add,
+            )
+            release_bank(("exch", g, i))
+
+        def take_direct(g, i):
+            y_sb[g, i] = kept("y%d_%d" % (g, i), [P, CHUNK], F32)
+            nc.vector.scalar_tensor_tensor(
+                out=y_sb[g, i][:], in0=held["direct", g, i][1][:], scalar=minus_lam[:, i : i + 1],
+                in1=partial[g, i][:], op0=ALU.mult, op1=ALU.add,
+            )
+            release_bank(("direct", g, i))
+            nc.sync.dma_start(out=out_0[rows(i), columns(g)], in_=y_sb[g, i][:])
+
+        def round_y(g, i):
+            y_pairs[g, i] = work.tile([P, CHUNK], BF16, name="y_pairs", bufs=6)
+            nc.scalar.copy(
+                out=y_pairs[g, i][:].rearrange("r (u p e) -> r u p e", u=2, e=2),
+                in_=y_sb[g, i][:].rearrange("r (p u e) -> r u p e", u=2, e=2),
+            )
+
+        def turn(g, i0, i1):
+            bank = take_bank(("turn", g, i0), [P, i1 - i0, 2, P])
+            for i in range(i0, i1):
+                words = y_pairs[g, i][:].bitcast(F32)
+                for u in range(2):
+                    nc.tensor.transpose(bank[:, i - i0, u, :], words[:, rows(u)], identity[:])
+
+        def unload(engine_copy, g, i0, i1):
+            if g not in y_grouped:
+                y_grouped[g] = work.tile([P, R * PACK], BF16, name="y_grouped", bufs=2, align_bytes=64)
+            words = y_grouped[g][:].bitcast(F32)[:, 2 * P * i0 : 2 * P * i1]
+            engine_copy(
+                out=words.rearrange("p (i r u) -> p i r u", r=P, u=2),
+                in_=held["turn", g, i0][1][:].rearrange("p i u r -> p i r u"),
+            )
+            release_bank(("turn", g, i0))
+
+        def quantise_y(g, i0, i1):
+            if g not in y_codes:
+                y_codes[g] = kept("y_codes%d" % g, [P, R], U32)
+            cols = slice(P * i0, P * i1)
+            nc.vector.quantize_mx(
+                out=y_codes[g][:, cols].bitcast(FP8X4),
+                scales=y_plane[4 * g :, cols],
+                in_=y_grouped[g][:, PACK * P * i0 : PACK * P * i1],
+            )
+            dst = out_1[g].rearrange("p m t -> p (m t)").bitcast(I32)
+            nc.sync.dma_start(out=dst[:, cols], in_=y_codes[g][:, cols].bitcast(I32))
+
+        minus_lam = kept("minus_lam", [P, TILES], F32)
+        last = CHUNKS - 1
+        for g in range(CHUNKS):
+            if g == 0:
+                for j in range(PASSES):
+                    for i in range(TILES):
+                        mx_pass("exch", 0, i, j)
+                for j in range(PASSES):
+                    interleave_scalar(0, j)
+                    interleave_vector(0, j)
+                    quantise_c(0, j)
+                nc.vector.tensor_scalar(
+                    out=minus_lam[:], in0=lam_sb[:, :, 0], scalar1=-1.0, scalar2=None, op0=ALU.mult
+                )
+                for j in range(PASSES - 1):
+                    for i in range(TILES):
+                        mx_pass("amp", 0, i, j)
+            else:
+                for i in range(TILES):
+                    product("exch", g, i)
+                interleave_scalar(g, 2)
+                interleave_vector(g, 2)
+                quantise_c(g, 1)
+                take_direct(g - 1, 1)
+                quantise_c(g, 2)
+                take_direct(g - 1, 2)
+                take_direct(g - 1, 3)
+                if g > 1:
+                    quantise_y(g - 2, 0, TILES)
+                for i in range(TILES):
+                    round_y(g - 1, i)
+            for i in range(TILES):
+                if g == 0:
+                    mx_pass("amp", 0, i, PASSES - 1)
+                else:
+                    product("amp", g, i)
+                take_amp(g, i)
+                if i > 0:
+                    take_exch(g, i - 1)
+            if g > 0:
+                turn(g - 1, 0, 2)
+                turn(g - 1, 2, 4)
+            if g < last:
+                interleave_scalar(g + 1, 0)
+            for i in range(TILES):
+                product("direct", g, i)
+                if i == 0 and g > 0:
+                    unload(nc.scalar.copy, g - 1, 0, 2)
+                    unload(nc.scalar.copy, g - 1, 2, 4)
+                if i == 0 and g < last:
+                    interleave_scalar(g + 1, 1)
+                if i == 1:
+                    take_exch(g, TILES - 1)
+                    if g < last:
+                        interleave_vector(g + 1, 0)
+                if i == 2 and g < last:
+                    quantise_c(g + 1, 0)
+                    interleave_vector(g + 1, 1)
+                if i == 0 or (g == last and i < TILES - 1):
+                    take_direct(g, i)
+                    if g == last:
+                        round_y(g, i)
+
+        turn(last, 0, 2)
+        take_direct(last, 3)
+        round_y(last, 3)
+        turn(last, 2, 3)
+        turn(last, 3, 4)
+        unload(nc.vector.tensor_copy, last, 0, 2)
+        quantise_y(last - 1, 0, TILES)
+        unload(nc.scalar.copy, last, 2, 3)
+        unload(nc.scalar.copy, last, 3, 4)
+        quantise_y(last, 0, 2)
+        quantise_y(last, 2, 4)
+        for q in range(QUADS):
+            nc.scalar.dma_start(
+                out=out_2[:, 4 * q : 4 * q + 4, :].bitcast(I32),
+                in_=y_plane[32 * q : 32 * q + 16, :].bitcast(I32),
+            )

@@ -21,10 +21,38 @@ PASSES = K // (P * PACK)
 CHUNK = 512
 CHUNKS = V // CHUNK
 TILES = R // P
-QUADS = 4
+LAST = CHUNKS - 1
+QUADS, QUAD = 4, 32
+LIVE = 4
 BANKS = 8
+FP4_BYTES = 2
 RUN = 4
-VECTOR_COLUMNS = (320, 192, 64, 64)
+FIRST_SHARE = 320
+LATER_SHARE = 128
+
+
+def vector_share(g, j):
+    if g == 0:
+        return FIRST_SHARE
+    if g == 1:
+        return LATER_SHARE * j
+    return LATER_SHARE if j == PASSES - 1 else 0
+
+
+def columns(g):
+    return slice(g * CHUNK, (g + 1) * CHUNK)
+
+
+def rows(i):
+    return slice(i * P, (i + 1) * P)
+
+
+def word_order(ap):
+    return ap.rearrange("r (p u e) -> r u p e", u=2, e=2)
+
+
+def as_halves(ap):
+    return ap.rearrange("r (u p e) -> r u p e", u=2, e=2)
 
 
 def tile_gap_scaled_pair_action_k3_kernel(
@@ -40,37 +68,36 @@ def tile_gap_scaled_pair_action_k3_kernel(
         def kept(name, shape, dtype):
             return keep.tile(shape, dtype, name=name, align_bytes=64)
 
-        def columns(g):
-            return slice(g * CHUNK, (g + 1) * CHUNK)
-
-        def rows(i):
-            return slice(i * P, (i + 1) * P)
-
-        def scale_plane(name, width):
-            plane = kept(name, [P, PASSES, width], U8)
+        def zeroed_plane(name, shape):
+            plane = kept(name, shape, U8)
             nc.vector.memset(plane[:].bitcast(U32), 0)
             return plane
 
-        def load_scales(plane, scales, cols):
-            for q in range(QUADS):
-                nc.sync.dma_start(
-                    out=plane[32 * q : 32 * q + 4, :, :].bitcast(I32),
-                    in_=scales[:, 4 * q : 4 * q + 4, cols].rearrange("j r n -> r j n").bitcast(I32),
-                )
-
-        z_plane = scale_plane("z_plane", R)
-        b_plane = {0: scale_plane("b_plane0", CHUNK)}
-        d_plane = kept("d_plane", [P, V], U8)
-        nc.vector.memset(d_plane[:].bitcast(U32), 0)
-        for g in range(1, CHUNKS):
-            b_plane[g] = scale_plane("b_plane%d" % g, CHUNK)
+        z_plane = zeroed_plane("z_plane", [P, PASSES, R])
+        b_plane = {0: zeroed_plane("b_plane0", [P, PASSES, CHUNK])}
+        lam_wide = kept("lam_wide", [P, P], F32)
+        nc.vector.memset(lam_wide[:], 0.0)
+        d_plane = zeroed_plane("d_plane", [P, V])
         identity = kept("identity", [P, P], F32)
         make_identity(nc, identity[:])
 
-        z_sb, d_sb, b_sb, c_raw, gap_sb = {}, {}, {}, {}, {}
+        for q in range(QUADS):
+            nc.gpsimd.dma_start(
+                out=d_plane[QUAD * q + LIVE : QUAD * q + LIVE * (PASSES + 1), :].bitcast(I32),
+                in_=d_scales[:, LIVE * q : LIVE * (q + 1), :].bitcast(I32),
+            )
+
+        z_sb, d_sb, b_sb, c_raw = {}, {}, {}, {}
         z_view = z_words.rearrange("j p n t -> p j (n t)")
         d_view = d_words.rearrange("j p n t -> p j (n t)")
         b_view = b_words.rearrange("j p n -> p j n")
+
+        def load_scales(plane, scales, cols):
+            for s in range(LIVE):
+                nc.sync.dma_start(
+                    out=plane[s:P:QUAD, :, :].bitcast(I32),
+                    in_=scales[:, s : QUADS * LIVE : LIVE, cols].rearrange("j q n -> q j n").bitcast(I32),
+                )
 
         def load_z(j):
             z_sb[j] = kept("z%d" % j, [P, R], U32)
@@ -82,64 +109,60 @@ def tile_gap_scaled_pair_action_k3_kernel(
             nc.sync.dma_start(out=d_sb[g][:].bitcast(I32), in_=src.bitcast(I32))
 
         def load_b(g, j0, j1):
-            words = kept("b%d_%d" % (g, j0), [P, j1 - j0, 2 * CHUNK], U8)
-            src = b_view[:, j0:j1, g * 2 * CHUNK : (g + 1) * 2 * CHUNK]
+            width = FP4_BYTES * CHUNK
+            words = kept("b%d_%d" % (g, j0), [P, j1 - j0, width], U8)
+            src = b_view[:, j0:j1, g * width : (g + 1) * width]
             nc.sync.dma_start(out=words[:].bitcast(I32), in_=src.bitcast(I32))
             for j in range(j0, j1):
                 b_sb[g, j] = words[:, j - j0, :]
 
         def load_c(g, j):
             c_raw[g, j] = kept("c%d_%d" % (g, j), [P, PACK, CHUNK], BF16)
-            src = c[j * P * PACK : (j + 1) * P * PACK, columns(g)].rearrange("(p t) v -> p t v", t=PACK)
-            nc.sync.dma_start(out=c_raw[g, j][:], in_=src)
+            src = c[j * P * PACK : (j + 1) * P * PACK, columns(g)]
+            nc.sync.dma_start(out=c_raw[g, j][:], in_=src.rearrange("(p t) v -> p t v", t=PACK))
 
-        def load_gap(g):
-            gap_sb[g] = kept("gap%d" % g, [P, CHUNK], BF16)
-            nc.sync.dma_start(out=gap_sb[g][:], in_=gap[columns(g)].partition_broadcast(P))
-
-        load_z(0)
-        load_b(0, 0, 1)
+        gap_rows = kept("gap_rows", [P, V // P], BF16)
+        nc.sync.dma_start(out=gap_rows[:], in_=gap.rearrange("(k s) -> k s", k=P))
+        lam_rows = kept("lam_rows", [TILES, P], BF16)
+        nc.sync.dma_start(out=lam_rows[:], in_=lam.rearrange("(i p) -> i p", p=P))
         load_scales(z_plane, z_scales, slice(0, R))
+        load_z(0)
+        load_b(0, 0, PASSES - 1)
         load_scales(b_plane[0], b_scales, columns(0))
-        load_z(1)
-        load_b(0, 1, PASSES)
-        load_c(0, 0)
-        load_z(2)
-        load_c(0, 1)
-        load_c(0, 2)
-        load_gap(0)
-        lam_sb = kept("lam_sb", [P, TILES, 2], BF16)
-        with nc.allow_non_contiguous_dma(reason="one coupling strength for each partition"):
-            nc.sync.dma_start(out=lam_sb[:, :, 0:1], in_=lam.rearrange("(i p o) -> p i o", p=P, o=1))
-        for q in range(QUADS):
-            nc.sync.dma_start(
-                out=d_plane[32 * q : 32 * q + 4 * PASSES, :].bitcast(I32),
-                in_=d_scales[:, 4 * q : 4 * q + 4, :].bitcast(I32),
-            )
+        for j in range(PASSES):
+            load_c(0, j)
+            if j + 1 < PASSES:
+                load_z(j + 1)
+        load_b(0, PASSES - 1, PASSES)
+
+        nc.vector.tensor_copy(out=lam_wide[0:TILES, :], in_=lam_rows[:])
+        for g in range(1, CHUNKS):
+            b_plane[g] = zeroed_plane("b_plane%d" % g, [P, PASSES, CHUNK])
+
         load_d(0)
         for g in range(1, CHUNKS):
+            load_c(g, 0)
             load_scales(b_plane[g], b_scales, columns(g))
             load_b(g, 0, PASSES)
-            for j in range(PASSES):
+            for j in range(1, PASSES):
                 load_c(g, j)
-            load_gap(g)
             load_d(g)
 
         grouped, c_codes, c_plane = {}, {}, {}
 
         def interleave(engine_copy, g, j, lo, hi):
             if (g, j) not in grouped:
-                grouped[g, j] = work.tile([P, CHUNK, PACK], BF16, name="grouped", bufs=4, align_bytes=64)
+                grouped[g, j] = work.tile([P, CHUNK, PACK], BF16, name="grouped", bufs=PASSES + 1, align_bytes=64)
             engine_copy(
                 out=grouped[g, j][:, lo:hi, :].rearrange("p (a i) t -> p a t i", i=RUN),
                 in_=c_raw[g, j][:, :, lo:hi].rearrange("p t (a i) -> p a t i", i=RUN),
             )
 
         def interleave_scalar(g, j):
-            interleave(nc.scalar.copy, g, j, VECTOR_COLUMNS[g], CHUNK)
+            interleave(nc.scalar.copy, g, j, vector_share(g, j), CHUNK)
 
         def interleave_vector(g, j):
-            interleave(nc.vector.tensor_copy, g, j, 0, VECTOR_COLUMNS[g])
+            interleave(nc.vector.tensor_copy, g, j, 0, vector_share(g, j))
 
         def quantise_c(g, j):
             c_codes[g, j] = kept("c_codes%d_%d" % (g, j), [P, CHUNK], U32)
@@ -151,26 +174,27 @@ def tile_gap_scaled_pair_action_k3_kernel(
             )
 
         free = list(range(BANKS))
-        held = {}
+        bank_number, bank_tile = {}, {}
 
         def take_bank(key, shape):
             n = free[0]
             free.remove(n)
-            held[key] = (n, psum.tile(shape, F32, name="bank%d" % n))
-            return held[key][1]
+            bank_number[key] = n
+            bank_tile[key] = psum.tile(shape, F32, name="bank%d" % n)
+            return bank_tile[key]
 
         def release_bank(key):
-            free.append(held[key][0])
+            free.append(bank_number[key])
 
         def moving(kind, g, j):
             if kind == "amp":
                 return c_codes[g, j][:].bitcast(FP8X4), c_plane[g, j][:]
             if kind == "direct":
-                return d_sb[g][:, j, :].bitcast(FP8X4), d_plane[4 * j :, columns(g)]
+                return d_sb[g][:, j, :].bitcast(FP8X4), d_plane[LIVE * (j + 1) :, columns(g)]
             return b_sb[g, j].bitcast(FP4X4), b_plane[g][:, j, :]
 
         def mx_pass(kind, g, i, j):
-            acc = take_bank((kind, g, i), [P, CHUNK]) if j == 0 else held[kind, g, i][1]
+            acc = take_bank((kind, g, i), [P, CHUNK]) if j == 0 else bank_tile[kind, g, i]
             codes, plane = moving(kind, g, j)
             nc.tensor.matmul_mx(
                 out=acc[:],
@@ -186,37 +210,46 @@ def tile_gap_scaled_pair_action_k3_kernel(
             for j in range(PASSES):
                 mx_pass(kind, g, i, j)
 
-        scaled, partial, y_sb, y_pairs, y_grouped, y_codes = {}, {}, {}, {}, {}, {}
-        y_plane = kept("y_plane", [P, R], U8)
+        scaled, partial, y_sb, y_wide = {}, {}, {}, {}
 
         def take_amp(g, i):
             scaled[g, i] = work.tile([P, CHUNK], F32, name="scaled")
-            nc.vector.tensor_tensor(out=scaled[g, i][:], in0=held["amp", g, i][1][:], in1=gap_sb[g][:], op=ALU.mult)
+            nc.vector.tensor_tensor(
+                out=scaled[g, i][:], in0=bank_tile["amp", g, i][:], in1=gap_all[:, columns(g)], op=ALU.mult
+            )
             release_bank(("amp", g, i))
 
         def take_exch(g, i):
-            partial[g, i] = work.tile([P, CHUNK], F32, name="partial", bufs=4)
+            partial[g, i] = work.tile([P, CHUNK], F32, name="partial", bufs=TILES)
             nc.vector.scalar_tensor_tensor(
-                out=partial[g, i][:], in0=held["exch", g, i][1][:], scalar=lam_sb[:, i, 0:1],
+                out=partial[g, i][:], in0=bank_tile["exch", g, i][:], scalar=plus_lam[:, i : i + 1],
                 in1=scaled[g, i][:], op0=ALU.mult, op1=ALU.add,
             )
             release_bank(("exch", g, i))
 
         def take_direct(g, i):
-            y_sb[g, i] = kept("y%d_%d" % (g, i), [P, CHUNK], F32)
+            if g == 0:
+                y_wide[i] = kept("y_wide%d" % i, [P, 2 * CHUNK], F32)
+            y_sb[g, i] = y_wide[i][:, columns(g)] if g < 2 else kept("y%d_%d" % (g, i), [P, CHUNK], F32)
             nc.vector.scalar_tensor_tensor(
-                out=y_sb[g, i][:], in0=held["direct", g, i][1][:], scalar=minus_lam[:, i : i + 1],
+                out=y_sb[g, i][:], in0=bank_tile["direct", g, i][:], scalar=minus_lam[:, i : i + 1],
                 in1=partial[g, i][:], op0=ALU.mult, op1=ALU.add,
             )
             release_bank(("direct", g, i))
-            nc.sync.dma_start(out=out_0[rows(i), columns(g)], in_=y_sb[g, i][:])
+            if g == 1:
+                nc.sync.dma_start(out=out_0[rows(i), 0 : 2 * CHUNK], in_=y_wide[i][:])
+            elif g > 1:
+                nc.sync.dma_start(out=out_0[rows(i), columns(g)], in_=y_sb[g, i][:])
+
+        y_pairs, y_grouped, y_codes = {}, {}, {}
+        y_plane = kept("y_plane", [P, R], U8)
+
+        def pairs_tile(g, i):
+            y_pairs[g, i] = work.tile([P, CHUNK], BF16, name="y_pairs", bufs=TILES + 2)
+            return y_pairs[g, i]
 
         def round_y(g, i):
-            y_pairs[g, i] = work.tile([P, CHUNK], BF16, name="y_pairs", bufs=6)
-            nc.scalar.copy(
-                out=y_pairs[g, i][:].rearrange("r (u p e) -> r u p e", u=2, e=2),
-                in_=y_sb[g, i][:].rearrange("r (p u e) -> r u p e", u=2, e=2),
-            )
+            nc.scalar.copy(out=as_halves(pairs_tile(g, i)[:]), in_=word_order(y_sb[g, i][:]))
 
         def turn(g, i0, i1):
             bank = take_bank(("turn", g, i0), [P, i1 - i0, 2, P])
@@ -225,15 +258,21 @@ def tile_gap_scaled_pair_action_k3_kernel(
                 for u in range(2):
                     nc.tensor.transpose(bank[:, i - i0, u, :], words[:, rows(u)], identity[:])
 
-        def unload(engine_copy, g, i0, i1):
+        def unload(g, i0, i1):
             if g not in y_grouped:
-                y_grouped[g] = work.tile([P, R * PACK], BF16, name="y_grouped", bufs=2, align_bytes=64)
+                y_grouped[g] = work.tile([P, R * PACK], BF16, name="y_grouped", align_bytes=64)
             words = y_grouped[g][:].bitcast(F32)[:, 2 * P * i0 : 2 * P * i1]
-            engine_copy(
+            nc.scalar.copy(
                 out=words.rearrange("p (i r u) -> p i r u", r=P, u=2),
-                in_=held["turn", g, i0][1][:].rearrange("p i u r -> p i r u"),
+                in_=bank_tile["turn", g, i0][:].rearrange("p i u r -> p i r u"),
             )
             release_bank(("turn", g, i0))
+
+        def turn_chunk(g):
+            turn(g, 0, 2)
+            turn(g, 2, TILES)
+            unload(g, 0, 2)
+            unload(g, 2, TILES)
 
         def quantise_y(g, i0, i1):
             if g not in y_codes:
@@ -241,29 +280,40 @@ def tile_gap_scaled_pair_action_k3_kernel(
             cols = slice(P * i0, P * i1)
             nc.vector.quantize_mx(
                 out=y_codes[g][:, cols].bitcast(FP8X4),
-                scales=y_plane[4 * g :, cols],
+                scales=y_plane[LIVE * g :, cols],
                 in_=y_grouped[g][:, PACK * P * i0 : PACK * P * i1],
             )
             dst = out_1[g].rearrange("p m t -> p (m t)").bitcast(I32)
             nc.sync.dma_start(out=dst[:, cols], in_=y_codes[g][:, cols].bitcast(I32))
 
+        gap_all = kept("gap_all", [P, V], BF16)
+        gap_words = gap_rows[:].bitcast(F32)
+        gap_out = gap_all[:].bitcast(F32).rearrange("m (k s) -> m k s", k=P)
+        per_bank = CHUNK // P
+        for s0 in range(0, V // (2 * P), per_bank):
+            bank = take_bank(("gap", s0), [P, per_bank, P])
+            for s in range(per_bank):
+                column = gap_words[:, s0 + s : s0 + s + 1]
+                nc.tensor.transpose(bank[:, s, :], column.to_broadcast([P, P]), identity[:])
+            nc.scalar.copy(out=gap_out[:, :, s0 : s0 + per_bank], in_=bank[:].rearrange("m s k -> m k s"))
+            release_bank(("gap", s0))
+        plus_lam = kept("plus_lam", [P, TILES], F32)
         minus_lam = kept("minus_lam", [P, TILES], F32)
-        last = CHUNKS - 1
-        for g in range(CHUNKS):
+        bank = take_bank("lam", [P, P])
+        nc.tensor.transpose(bank[:], lam_wide[:], identity[:])
+        nc.vector.tensor_copy(out=plus_lam[:], in_=bank[:, 0:TILES])
+        nc.vector.tensor_scalar(out=minus_lam[:], in0=bank[:, 0:TILES], scalar1=-1.0, scalar2=None, op0=ALU.mult)
+        release_bank("lam")
+
+        for g in range(LAST):
             if g == 0:
-                for j in range(PASSES):
-                    for i in range(TILES):
-                        mx_pass("exch", 0, i, j)
                 for j in range(PASSES):
                     interleave_scalar(0, j)
                     interleave_vector(0, j)
                     quantise_c(0, j)
-                nc.vector.tensor_scalar(
-                    out=minus_lam[:], in0=lam_sb[:, :, 0], scalar1=-1.0, scalar2=None, op0=ALU.mult
-                )
-                for j in range(PASSES - 1):
+                for kind, j in (("exch", 0), ("exch", 1), ("amp", 0), ("amp", 1), ("exch", 2)):
                     for i in range(TILES):
-                        mx_pass("amp", 0, i, j)
+                        mx_pass(kind, 0, i, j)
             else:
                 for i in range(TILES):
                     product("exch", g, i)
@@ -271,13 +321,21 @@ def tile_gap_scaled_pair_action_k3_kernel(
                 interleave_vector(g, 2)
                 quantise_c(g, 1)
                 take_direct(g - 1, 1)
-                quantise_c(g, 2)
-                take_direct(g - 1, 2)
-                take_direct(g - 1, 3)
-                if g > 1:
+                if g == 1:
+                    quantise_c(g, 2)
+                    take_direct(g - 1, 2)
+                else:
+                    take_direct(g - 1, 2)
                     quantise_y(g - 2, 0, TILES)
-                for i in range(TILES):
-                    round_y(g - 1, i)
+                    quantise_c(g, 2)
+                take_direct(g - 1, 3)
+                round_y(g - 1, 0)
+                round_y(g - 1, 1)
+            interleave_scalar(g + 1, 0)
+            if g == 1:
+                round_y(0, 2)
+                round_y(0, 3)
+            interleave_scalar(g + 1, 1)
             for i in range(TILES):
                 if g == 0:
                     mx_pass("amp", 0, i, PASSES - 1)
@@ -286,43 +344,69 @@ def tile_gap_scaled_pair_action_k3_kernel(
                 take_amp(g, i)
                 if i > 0:
                     take_exch(g, i - 1)
-            if g > 0:
-                turn(g - 1, 0, 2)
-                turn(g - 1, 2, 4)
-            if g < last:
-                interleave_scalar(g + 1, 0)
-            for i in range(TILES):
-                product("direct", g, i)
-                if i == 0 and g > 0:
-                    unload(nc.scalar.copy, g - 1, 0, 2)
-                    unload(nc.scalar.copy, g - 1, 2, 4)
-                if i == 0 and g < last:
-                    interleave_scalar(g + 1, 1)
-                if i == 1:
-                    take_exch(g, TILES - 1)
-                    if g < last:
-                        interleave_vector(g + 1, 0)
-                if i == 2 and g < last:
-                    quantise_c(g + 1, 0)
-                    interleave_vector(g + 1, 1)
-                if i == 0 or (g == last and i < TILES - 1):
-                    take_direct(g, i)
-                    if g == last:
-                        round_y(g, i)
+            product("direct", g, 0)
+            take_direct(g, 0)
+            product("direct", g, 1)
+            take_exch(g, 3)
+            if g == 1:
+                turn_chunk(0)
+            product("direct", g, 2)
+            quantise_c(g + 1, 0)
+            if g == 0:
+                interleave_vector(1, 1)
+            product("direct", g, 3)
 
-        turn(last, 0, 2)
-        take_direct(last, 3)
-        round_y(last, 3)
-        turn(last, 2, 3)
-        turn(last, 3, 4)
-        unload(nc.vector.tensor_copy, last, 0, 2)
-        quantise_y(last - 1, 0, TILES)
-        unload(nc.scalar.copy, last, 2, 3)
-        unload(nc.scalar.copy, last, 3, 4)
-        quantise_y(last, 0, 2)
-        quantise_y(last, 2, 4)
+        product("exch", LAST, 0)
+        product("exch", LAST, 1)
+        interleave_scalar(LAST, 2)
+        interleave_vector(LAST, 2)
+        round_y(LAST - 2, 2)
+        round_y(LAST - 2, 3)
+        turn_chunk(LAST - 2)
+        quantise_c(LAST, 1)
+        take_direct(LAST - 1, 1)
+        quantise_c(LAST, 2)
+        take_direct(LAST - 1, 2)
+        take_direct(LAST - 1, 3)
+        for i in range(TILES):
+            round_y(LAST - 1, i)
+        for i in range(TILES):
+            product("amp", LAST, i)
+            if i == 3:
+                turn(LAST, 0, 2)
+                unload(LAST, 0, 2)
+            if i > 1:
+                product("exch", LAST, i)
+            product("direct", LAST, i)
+            take_amp(LAST, i)
+            if i > 0:
+                take_direct(LAST, i - 1)
+                round_y(LAST, i - 1)
+            take_exch(LAST, i)
+            if i == 0:
+                quantise_y(LAST - 2, 0, TILES)
+            if i == 1:
+                turn_chunk(LAST - 1)
+            if i == 2:
+                quantise_y(LAST - 1, 0, TILES)
+
+        quantise_y(LAST, 0, 2)
+        turn(LAST, 2, 3)
+        halves = as_halves(pairs_tile(LAST, 3)[:])
+        for u in range(2):
+            nc.vector.scalar_tensor_tensor(
+                out=halves[:, u], in0=word_order(bank_tile["direct", LAST, 3][:])[:, u], scalar=minus_lam[:, 3:4],
+                in1=word_order(partial[LAST, 3][:])[:, u], op0=ALU.mult, op1=ALU.add,
+            )
+        turn(LAST, 3, 4)
+        take_direct(LAST, 3)
+        unload(LAST, 2, 3)
+        unload(LAST, 3, 4)
+        quantise_y(LAST, 2, 3)
+        quantise_y(LAST, 3, 4)
         for q in range(QUADS):
-            nc.scalar.dma_start(
-                out=out_2[:, 4 * q : 4 * q + 4, :].bitcast(I32),
-                in_=y_plane[32 * q : 32 * q + 16, :].bitcast(I32),
+            queue = nc.scalar if q % 2 == 0 else nc.sync
+            queue.dma_start(
+                out=out_2[:, LIVE * q : LIVE * (q + 1), :].bitcast(I32),
+                in_=y_plane[QUAD * q : QUAD * q + LIVE * CHUNKS, :].bitcast(I32),
             )

@@ -26,6 +26,7 @@ QUADS, QUAD = 4, 32
 LIVE = 4
 BANKS = 8
 FP4_BYTES = 2
+ALIGN = 256
 RUN = 4
 FIRST_SHARE = 320
 LATER_SHARE = 128
@@ -66,7 +67,9 @@ def tile_gap_scaled_pair_action_k3_kernel(
         ctx.enter_context(tc.manual_schedule())
 
         def kept(name, shape, dtype):
-            return keep.tile(shape, dtype, name=name, align_bytes=64)
+            if dtype in (U32, U8):
+                return keep.tile(shape, dtype, name=name, align_bytes=ALIGN)
+            return keep.tile(shape, dtype, name=name)
 
         def zeroed_plane(name, shape):
             plane = kept(name, shape, U8)
@@ -77,15 +80,9 @@ def tile_gap_scaled_pair_action_k3_kernel(
         b_plane = {0: zeroed_plane("b_plane0", [P, PASSES, CHUNK])}
         lam_wide = kept("lam_wide", [P, P], F32)
         nc.vector.memset(lam_wide[:], 0.0)
-        d_plane = zeroed_plane("d_plane", [P, V])
+        d_plane = {0: zeroed_plane("d_plane0", [P, PASSES, CHUNK])}
         identity = kept("identity", [P, P], F32)
         make_identity(nc, identity[:])
-
-        for q in range(QUADS):
-            nc.gpsimd.dma_start(
-                out=d_plane[QUAD * q + LIVE : QUAD * q + LIVE * (PASSES + 1), :].bitcast(I32),
-                in_=d_scales[:, LIVE * q : LIVE * (q + 1), :].bitcast(I32),
-            )
 
         z_sb, d_sb, b_sb, c_raw = {}, {}, {}, {}
         z_view = z_words.rearrange("j p n t -> p j (n t)")
@@ -129,16 +126,19 @@ def tile_gap_scaled_pair_action_k3_kernel(
         load_z(0)
         load_b(0, 0, PASSES - 1)
         load_scales(b_plane[0], b_scales, columns(0))
-        for j in range(PASSES):
-            load_c(0, j)
-            if j + 1 < PASSES:
-                load_z(j + 1)
+        load_c(0, 0)
+        load_z(1)
+        load_c(0, 1)
+        load_c(0, 2)
+        load_z(2)
         load_b(0, PASSES - 1, PASSES)
 
         nc.vector.tensor_copy(out=lam_wide[0:TILES, :], in_=lam_rows[:])
         for g in range(1, CHUNKS):
             b_plane[g] = zeroed_plane("b_plane%d" % g, [P, PASSES, CHUNK])
+            d_plane[g] = zeroed_plane("d_plane%d" % g, [P, PASSES, CHUNK])
 
+        load_scales(d_plane[0], d_scales, columns(0))
         load_d(0)
         for g in range(1, CHUNKS):
             load_c(g, 0)
@@ -146,13 +146,14 @@ def tile_gap_scaled_pair_action_k3_kernel(
             load_b(g, 0, PASSES)
             for j in range(1, PASSES):
                 load_c(g, j)
+            load_scales(d_plane[g], d_scales, columns(g))
             load_d(g)
 
         grouped, c_codes, c_plane = {}, {}, {}
 
         def interleave(engine_copy, g, j, lo, hi):
             if (g, j) not in grouped:
-                grouped[g, j] = work.tile([P, CHUNK, PACK], BF16, name="grouped", bufs=PASSES + 1, align_bytes=64)
+                grouped[g, j] = work.tile([P, CHUNK, PACK], BF16, name="grouped", bufs=PASSES + 1, align_bytes=ALIGN)
             engine_copy(
                 out=grouped[g, j][:, lo:hi, :].rearrange("p (a i) t -> p a t i", i=RUN),
                 in_=c_raw[g, j][:, :, lo:hi].rearrange("p t (a i) -> p a t i", i=RUN),
@@ -190,7 +191,7 @@ def tile_gap_scaled_pair_action_k3_kernel(
             if kind == "amp":
                 return c_codes[g, j][:].bitcast(FP8X4), c_plane[g, j][:]
             if kind == "direct":
-                return d_sb[g][:, j, :].bitcast(FP8X4), d_plane[LIVE * (j + 1) :, columns(g)]
+                return d_sb[g][:, j, :].bitcast(FP8X4), d_plane[g][:, j, :]
             return b_sb[g, j].bitcast(FP4X4), b_plane[g][:, j, :]
 
         def mx_pass(kind, g, i, j):
@@ -260,7 +261,7 @@ def tile_gap_scaled_pair_action_k3_kernel(
 
         def unload(g, i0, i1):
             if g not in y_grouped:
-                y_grouped[g] = work.tile([P, R * PACK], BF16, name="y_grouped", align_bytes=64)
+                y_grouped[g] = work.tile([P, R * PACK], BF16, name="y_grouped", bufs=2, align_bytes=ALIGN)
             words = y_grouped[g][:].bitcast(F32)[:, 2 * P * i0 : 2 * P * i1]
             nc.scalar.copy(
                 out=words.rearrange("p (i r u) -> p i r u", r=P, u=2),
@@ -372,9 +373,6 @@ def tile_gap_scaled_pair_action_k3_kernel(
             round_y(LAST - 1, i)
         for i in range(TILES):
             product("amp", LAST, i)
-            if i == 3:
-                turn(LAST, 0, 2)
-                unload(LAST, 0, 2)
             if i > 1:
                 product("exch", LAST, i)
             product("direct", LAST, i)
@@ -390,8 +388,9 @@ def tile_gap_scaled_pair_action_k3_kernel(
             if i == 2:
                 quantise_y(LAST - 1, 0, TILES)
 
-        quantise_y(LAST, 0, 2)
+        turn(LAST, 0, 2)
         turn(LAST, 2, 3)
+        unload(LAST, 0, 2)
         halves = as_halves(pairs_tile(LAST, 3)[:])
         for u in range(2):
             nc.vector.scalar_tensor_tensor(
@@ -402,6 +401,7 @@ def tile_gap_scaled_pair_action_k3_kernel(
         take_direct(LAST, 3)
         unload(LAST, 2, 3)
         unload(LAST, 3, 4)
+        quantise_y(LAST, 0, 2)
         quantise_y(LAST, 2, 3)
         quantise_y(LAST, 3, 4)
         for q in range(QUADS):

from contextlib import ExitStack

import concourse.mybir as mybir
from concourse.masks import make_identity

R, K, V = 512, 1536, 2048
FLOPS = 3 * 2 * R * K * V

F32 = mybir.dt.float32
BF16 = mybir.dt.bfloat16
I32 = mybir.dt.int32
U32 = mybir.dt.uint32
U8 = mybir.dt.uint8
FP8X4 = mybir.dt.float8_e4m3fn_x4
FP4X4 = mybir.dt.float4_e2m1fn_x4
ALU = mybir.AluOpType

P = 128
PACK = 4
PASSES = K // (P * PACK)
CHUNK = 512
CHUNKS = V // CHUNK
TILES = R // P
LAST = CHUNKS - 1
QUADS, QUAD = 4, 32
LIVE = 4
BANKS = 8
FP4_BYTES = 2
ALIGN = 256
RUN = 4
FIRST_SHARE = 320
LATER_SHARE = 128


def vector_share(g, j):
    if g == 0:
        return FIRST_SHARE
    if g == 1:
        return LATER_SHARE * j
    return LATER_SHARE if j == PASSES - 1 else 0


def columns(g):
    return slice(g * CHUNK, (g + 1) * CHUNK)


def rows(i):
    return slice(i * P, (i + 1) * P)


def word_order(ap):
    return ap.rearrange("r (p u e) -> r u p e", u=2, e=2)


def as_halves(ap):
    return ap.rearrange("r (u p e) -> r u p e", u=2, e=2)


def tile_gap_scaled_pair_action_k3_kernel(
    tc, z_words, z_scales, c, b_words, b_scales, d_words, d_scales, gap, lam, out_0, out_1, out_2
):
    nc = tc.nc
    with ExitStack() as ctx:
        keep = ctx.enter_context(tc.tile_pool(name="keep", bufs=1))
        work = ctx.enter_context(tc.tile_pool(name="work", bufs=3))
        psum = ctx.enter_context(tc.psum_pool(name="psum", bufs=1))
        ctx.enter_context(tc.manual_schedule())

        def kept(name, shape, dtype):
            if dtype in (U32, U8):
                return keep.tile(shape, dtype, name=name, align_bytes=ALIGN)
            return keep.tile(shape, dtype, name=name)

        def zeroed_plane(name, shape):
            plane = kept(name, shape, U8)
            nc.vector.memset(plane[:].bitcast(U32), 0)
            return plane

        z_plane = zeroed_plane("z_plane", [P, PASSES, R])
        b_plane = {0: zeroed_plane("b_plane0", [P, PASSES, CHUNK])}
        lam_wide = kept("lam_wide", [P, P], F32)
        nc.vector.memset(lam_wide[:], 0.0)
        d_plane = {0: zeroed_plane("d_plane0", [P, PASSES, CHUNK])}
        identity = kept("identity", [P, P], F32)
        make_identity(nc, identity[:])

        z_sb, d_sb, b_sb, c_raw = {}, {}, {}, {}
        z_view = z_words.rearrange("j p n t -> p j (n t)")
        d_view = d_words.rearrange("j p n t -> p j (n t)")
        b_view = b_words.rearrange("j p n -> p j n")

        def load_scales(plane, scales, cols):
            for s in range(LIVE):
                nc.sync.dma_start(
                    out=plane[s:P:QUAD, :, :].bitcast(I32),
                    in_=scales[:, s : QUADS * LIVE : LIVE, cols].rearrange("j q n -> q j n").bitcast(I32),
                )

        def load_z(j):
            z_sb[j] = kept("z%d" % j, [P, R], U32)
            nc.sync.dma_start(out=z_sb[j][:].bitcast(I32), in_=z_view[:, j, :].bitcast(I32))

        def load_d(g):
            d_sb[g] = kept("d%d" % g, [P, PASSES, CHUNK], U32)
            src = d_view[:, :, g * CHUNK * PACK : (g + 1) * CHUNK * PACK]
            nc.sync.dma_start(out=d_sb[g][:].bitcast(I32), in_=src.bitcast(I32))

        def load_b(g, j0, j1):
            width = FP4_BYTES * CHUNK
            words = kept("b%d_%d" % (g, j0), [P, j1 - j0, width], U8)
            src = b_view[:, j0:j1, g * width : (g + 1) * width]
            nc.sync.dma_start(out=words[:].bitcast(I32), in_=src.bitcast(I32))
            for j in range(j0, j1):
                b_sb[g, j] = words[:, j - j0, :]

        def load_c(g, j):
            c_raw[g, j] = kept("c%d_%d" % (g, j), [P, PACK, CHUNK], BF16)
            src = c[j * P * PACK : (j + 1) * P * PACK, columns(g)]
            nc.sync.dma_start(out=c_raw[g, j][:], in_=src.rearrange("(p t) v -> p t v", t=PACK))

        gap_rows = kept("gap_rows", [P, V // P], BF16)
        nc.sync.dma_start(out=gap_rows[:], in_=gap.rearrange("(k s) -> k s", k=P))
        lam_rows = kept("lam_rows", [TILES, P], BF16)
        nc.sync.dma_start(out=lam_rows[:], in_=lam.rearrange("(i p) -> i p", p=P))
        load_scales(z_plane, z_scales, slice(0, R))
        load_z(0)
        load_b(0, 0, PASSES - 1)
        load_scales(b_plane[0], b_scales, columns(0))
        load_c(0, 0)
        load_z(1)
        load_c(0, 1)
        load_c(0, 2)
        load_z(2)
        load_b(0, PASSES - 1, PASSES)

        nc.vector.tensor_copy(out=lam_wide[0:TILES, :], in_=lam_rows[:])
        for g in range(1, CHUNKS):
            b_plane[g] = zeroed_plane("b_plane%d" % g, [P, PASSES, CHUNK])
            d_plane[g] = zeroed_plane("d_plane%d" % g, [P, PASSES, CHUNK])

        load_scales(d_plane[0], d_scales, columns(0))
        load_d(0)
        for g in range(1, CHUNKS):
            load_c(g, 0)
            load_scales(b_plane[g], b_scales, columns(g))
            load_b(g, 0, PASSES)
            for j in range(1, PASSES):
                load_c(g, j)
            load_scales(d_plane[g], d_scales, columns(g))
            load_d(g)

        grouped, c_codes, c_plane = {}, {}, {}

        def interleave(engine_copy, g, j, lo, hi):
            if (g, j) not in grouped:
                grouped[g, j] = work.tile([P, CHUNK, PACK], BF16, name="grouped", bufs=PASSES + 1, align_bytes=ALIGN)
            engine_copy(
                out=grouped[g, j][:, lo:hi, :].rearrange("p (a i) t -> p a t i", i=RUN),
                in_=c_raw[g, j][:, :, lo:hi].rearrange("p t (a i) -> p a t i", i=RUN),
            )

        def interleave_scalar(g, j):
            interleave(nc.scalar.copy, g, j, vector_share(g, j), CHUNK)

        def interleave_vector(g, j):
            interleave(nc.vector.tensor_copy, g, j, 0, vector_share(g, j))

        def quantise_c(g, j):
            c_codes[g, j] = kept("c_codes%d_%d" % (g, j), [P, CHUNK], U32)
            c_plane[g, j] = kept("c_plane%d_%d" % (g, j), [P, CHUNK], U8)
            nc.vector.quantize_mx(
                out=c_codes[g, j][:].bitcast(FP8X4),
                scales=c_plane[g, j][:],
                in_=grouped[g, j][:].rearrange("p v t -> p (v t)"),
            )

        free = list(range(BANKS))
        bank_number, bank_tile = {}, {}

        def take_bank(key, shape):
            n = free[0]
            free.remove(n)
            bank_number[key] = n
            bank_tile[key] = psum.tile(shape, F32, name="bank%d" % n)
            return bank_tile[key]

        def release_bank(key):
            free.append(bank_number[key])

        def moving(kind, g, j):
            if kind == "amp":
                return c_codes[g, j][:].bitcast(FP8X4), c_plane[g, j][:]
            if kind == "direct":
                return d_sb[g][:, j, :].bitcast(FP8X4), d_plane[g][:, j, :]
            return b_sb[g, j].bitcast(FP4X4), b_plane[g][:, j, :]

        def mx_pass(kind, g, i, j):
            acc = take_bank((kind, g, i), [P, CHUNK]) if j == 0 else bank_tile[kind, g, i]
            codes, plane = moving(kind, g, j)
            nc.tensor.matmul_mx(
                out=acc[:],
                lhsT=z_sb[j][:, rows(i)].bitcast(FP8X4),
                lhsT_scale=z_plane[:, j, rows(i)],
                rhs=codes,
                rhs_scale=plane,
                start=(j == 0),
                stop=(j == PASSES - 1),
            )

        def product(kind, g, i):
            for j in range(PASSES):
                mx_pass(kind, g, i, j)

        scaled, partial, y_sb, y_wide = {}, {}, {}, {}

        def take_amp(g, i):
            scaled[g, i] = work.tile([P, CHUNK], F32, name="scaled")
            nc.vector.tensor_tensor(
                out=scaled[g, i][:], in0=bank_tile["amp", g, i][:], in1=gap_all[:, columns(g)], op=ALU.mult
            )
            release_bank(("amp", g, i))

        def take_exch(g, i):
            partial[g, i] = work.tile([P, CHUNK], F32, name="partial", bufs=TILES)
            nc.vector.scalar_tensor_tensor(
                out=partial[g, i][:], in0=bank_tile["exch", g, i][:], scalar=plus_lam[:, i : i + 1],
                in1=scaled[g, i][:], op0=ALU.mult, op1=ALU.add,
            )
            release_bank(("exch", g, i))

        def take_direct(g, i):
            if g == 0:
                y_wide[i] = kept("y_wide%d" % i, [P, 2 * CHUNK], F32)
            y_sb[g, i] = y_wide[i][:, columns(g)] if g < 2 else kept("y%d_%d" % (g, i), [P, CHUNK], F32)
            nc.vector.scalar_tensor_tensor(
                out=y_sb[g, i][:], in0=bank_tile["direct", g, i][:], scalar=minus_lam[:, i : i + 1],
                in1=partial[g, i][:], op0=ALU.mult, op1=ALU.add,
            )
            release_bank(("direct", g, i))
            if g == 1:
                nc.sync.dma_start(out=out_0[rows(i), 0 : 2 * CHUNK], in_=y_wide[i][:])
            elif g > 1:
                nc.sync.dma_start(out=out_0[rows(i), columns(g)], in_=y_sb[g, i][:])

        y_pairs, y_grouped, y_codes = {}, {}, {}
        y_plane = kept("y_plane", [P, R], U8)

        def pairs_tile(g, i):
            y_pairs[g, i] = work.tile([P, CHUNK], BF16, name="y_pairs", bufs=TILES + 2)
            return y_pairs[g, i]

        def round_y(g, i):
            nc.scalar.copy(out=as_halves(pairs_tile(g, i)[:]), in_=word_order(y_sb[g, i][:]))

        def turn(g, i0, i1):
            bank = take_bank(("turn", g, i0), [P, i1 - i0, 2, P])
            for i in range(i0, i1):
                words = y_pairs[g, i][:].bitcast(F32)
                for u in range(2):
                    nc.tensor.transpose(bank[:, i - i0, u, :], words[:, rows(u)], identity[:])

        def unload(g, i0, i1):
            if g not in y_grouped:
                y_grouped[g] = work.tile([P, R * PACK], BF16, name="y_grouped", bufs=2, align_bytes=ALIGN)
            words = y_grouped[g][:].bitcast(F32)[:, 2 * P * i0 : 2 * P * i1]
            nc.scalar.copy(
                out=words.rearrange("p (i r u) -> p i r u", r=P, u=2),
                in_=bank_tile["turn", g, i0][:].rearrange("p i u r -> p i r u"),
            )
            release_bank(("turn", g, i0))

        def turn_chunk(g):
            turn(g, 0, 2)
            turn(g, 2, TILES)
            unload(g, 0, 2)
            unload(g, 2, TILES)

        def quantise_y(g, i0, i1):
            if g not in y_codes:
                y_codes[g] = kept("y_codes%d" % g, [P, R], U32)
            cols = slice(P * i0, P * i1)
            nc.vector.quantize_mx(
                out=y_codes[g][:, cols].bitcast(FP8X4),
                scales=y_plane[LIVE * g :, cols],
                in_=y_grouped[g][:, PACK * P * i0 : PACK * P * i1],
            )
            dst = out_1[g].rearrange("p m t -> p (m t)").bitcast(I32)
            nc.sync.dma_start(out=dst[:, cols], in_=y_codes[g][:, cols].bitcast(I32))

        gap_all = kept("gap_all", [P, V], BF16)
        gap_words = gap_rows[:].bitcast(F32)
        gap_out = gap_all[:].bitcast(F32).rearrange("m (k s) -> m k s", k=P)
        per_bank = CHUNK // P
        for s0 in range(0, V // (2 * P), per_bank):
            bank = take_bank(("gap", s0), [P, per_bank, P])
            for s in range(per_bank):
                column = gap_words[:, s0 + s : s0 + s + 1]
                nc.tensor.transpose(bank[:, s, :], column.to_broadcast([P, P]), identity[:])
            nc.scalar.copy(out=gap_out[:, :, s0 : s0 + per_bank], in_=bank[:].rearrange("m s k -> m k s"))
            release_bank(("gap", s0))
        plus_lam = kept("plus_lam", [P, TILES], F32)
        minus_lam = kept("minus_lam", [P, TILES], F32)
        bank = take_bank("lam", [P, P])
        nc.tensor.transpose(bank[:], lam_wide[:], identity[:])
        nc.vector.tensor_copy(out=plus_lam[:], in_=bank[:, 0:TILES])
        nc.vector.tensor_scalar(out=minus_lam[:], in0=bank[:, 0:TILES], scalar1=-1.0, scalar2=None, op0=ALU.mult)
        release_bank("lam")

        for g in range(LAST):
            if g == 0:
                for j in range(PASSES):
                    interleave_scalar(0, j)
                    interleave_vector(0, j)
                    quantise_c(0, j)
                for kind, j in (("exch", 0), ("exch", 1), ("amp", 0), ("amp", 1), ("exch", 2)):
                    for i in range(TILES):
                        mx_pass(kind, 0, i, j)
            else:
                for i in range(TILES):
                    product("exch", g, i)
                interleave_scalar(g, 2)
                interleave_vector(g, 2)
                quantise_c(g, 1)
                take_direct(g - 1, 1)
                if g == 1:
                    quantise_c(g, 2)
                    take_direct(g - 1, 2)
                else:
                    take_direct(g - 1, 2)
                    quantise_y(g - 2, 0, TILES)
                    quantise_c(g, 2)
                take_direct(g - 1, 3)
                round_y(g - 1, 0)
                round_y(g - 1, 1)
            interleave_scalar(g + 1, 0)
            if g == 1:
                round_y(0, 2)
                round_y(0, 3)
            interleave_scalar(g + 1, 1)
            for i in range(TILES):
                if g == 0:
                    mx_pass("amp", 0, i, PASSES - 1)
                else:
                    product("amp", g, i)
                take_amp(g, i)
                if i > 0:
                    take_exch(g, i - 1)
            product("direct", g, 0)
            take_direct(g, 0)
            product("direct", g, 1)
            take_exch(g, 3)
            if g == 1:
                turn_chunk(0)
            product("direct", g, 2)
            quantise_c(g + 1, 0)
            if g == 0:
                interleave_vector(1, 1)
            product("direct", g, 3)

        product("exch", LAST, 0)
        product("exch", LAST, 1)
        interleave_scalar(LAST, 2)
        interleave_vector(LAST, 2)
        round_y(LAST - 2, 2)
        round_y(LAST - 2, 3)
        turn_chunk(LAST - 2)
        quantise_c(LAST, 1)
        take_direct(LAST - 1, 1)
        quantise_c(LAST, 2)
        take_direct(LAST - 1, 2)
        take_direct(LAST - 1, 3)
        for i in range(TILES):
            round_y(LAST - 1, i)
        for i in range(TILES):
            product("amp", LAST, i)
            if i > 1:
                product("exch", LAST, i)
            product("direct", LAST, i)
            take_amp(LAST, i)
            if i > 0:
                take_direct(LAST, i - 1)
                round_y(LAST, i - 1)
            take_exch(LAST, i)
            if i == 0:
                quantise_y(LAST - 2, 0, TILES)
            if i == 1:
                turn_chunk(LAST - 1)
            if i == 2:
                quantise_y(LAST - 1, 0, TILES)

        turn(LAST, 0, 2)
        turn(LAST, 2, 3)
        unload(LAST, 0, 2)
        halves = as_halves(pairs_tile(LAST, 3)[:])
        for u in range(2):
            nc.vector.scalar_tensor_tensor(
                out=halves[:, u], in0=word_order(bank_tile["direct", LAST, 3][:])[:, u], scalar=minus_lam[:, 3:4],
                in1=word_order(partial[LAST, 3][:])[:, u], op0=ALU.mult, op1=ALU.add,
            )
        turn(LAST, 3, 4)
        take_direct(LAST, 3)
        unload(LAST, 2, 3)
        unload(LAST, 3, 4)
        quantise_y(LAST, 0, 2)
        quantise_y(LAST, 2, 3)
        quantise_y(LAST, 3, 4)
        for q in range(QUADS):
            queue = nc.scalar if q % 2 == 0 else nc.sync
            queue.dma_start(
                out=out_2[:, LIVE * q : LIVE * (q + 1), :].bitcast(I32),
                in_=y_plane[QUAD * q : QUAD * q + LIVE * CHUNKS, :].bitcast(I32),
            )
